import numpy as np
import ml_dtypes


def mxq(x, axis, fmt="e4m3"):
    dtype, down = {"e4m3": (ml_dtypes.float8_e4m3fn, 7), "e5m2": (ml_dtypes.float8_e5m2, 14)}[fmt]
    v = np.moveaxis(np.asarray(x, np.float32).astype(ml_dtypes.bfloat16).astype(np.float64), axis, -1)
    blocks = v.reshape(v.shape[:-1] + (-1, 32))
    amax = np.abs(blocks).max(-1, keepdims=True)
    byte = np.maximum(np.where(amax > 0, np.frexp(amax)[1] - 1 + 127, 0) - down, 1)
    scale = np.exp2(byte - 127.0)
    codes = (blocks / scale).astype(np.float32).astype(dtype).astype(np.float64)
    return np.moveaxis((codes * scale).reshape(v.shape), -1, axis)


WIDE = False


def mx_kscale(k):
    if not WIDE:
        return np.ones(k)
    levels = np.array([10, -10, 5, -5, 0])
    if k % 512:
        return np.exp2(np.random.permutation(np.resize(levels, k // 32))).repeat(32)
    a = np.empty((k // 512, 16))
    for p in range(k // 512):
        a[p, :8] = np.random.permutation(np.resize(levels, 8))
        for g in range(8):
            far = levels[np.abs(levels - a[p, g]) >= 10]
            a[p, g + 8] = far[np.random.randint(len(far))]
    return np.exp2(a.ravel()).repeat(32)


def f64(x):
    return np.asarray(x).astype(np.float64)


def striped(idx):
    return np.tile(idx.reshape(-1, 16).T, (8, 1)).astype(np.uint16)


def unstriped(offs):
    return offs[:16].T.reshape(-1).astype(np.int64)


E2M1 = np.array([0.0, 0.5, 1.0, 1.5, 2.0, 3.0, 4.0, 6.0, -0.0, -0.5, -1.0, -1.5, -2.0, -3.0, -4.0, -6.0])


def pack_weight(w, fmt):
    k, n = w.shape
    w = f64(np.asarray(w, np.float32).astype(ml_dtypes.bfloat16)).reshape(k // 32, 32, n)
    amax = np.abs(w).max(1)
    if fmt == "e4m3":
        byte = np.frexp(amax)[1] - 1 + 127 - 7
    else:
        mant, ex = np.frexp(amax / 6.0)
        byte = np.where(mant > 0.5, ex, ex - 1) + 127
    byte = np.clip(np.where(amax > 0, byte, 1), 1, 254)
    scaled = (w * np.exp2(127.0 - byte)[:, None, :]).reshape(k, n).astype(np.float32)
    by_word = np.ascontiguousarray(scaled.reshape(k // 512, 128, 4, n).transpose(0, 1, 3, 2))
    if fmt == "e4m3":
        words = by_word.astype(ml_dtypes.float8_e4m3fn).view(np.uint8)
    else:
        c = by_word.astype(ml_dtypes.float4_e2m1fn).view(np.uint8) & 0xF
        words = (c[..., 0::2] | (c[..., 1::2] << 4)).reshape(k // 512, 128, 2 * n)
    return np.ascontiguousarray(words), np.ascontiguousarray(byte.astype(np.uint8).reshape(k // 512, 16, n))


def unpack_weight(words, scales, fmt):
    g, _, n = scales.shape
    words = np.ascontiguousarray(words).reshape(g, 128, n, -1)
    if fmt == "e4m3":
        vals = words.view(ml_dtypes.float8_e4m3fn).astype(np.float64)
    else:
        nib = np.empty((g, 128, n, 4), np.uint8)
        nib[..., 0::2] = words & 0xF
        nib[..., 1::2] = words >> 4
        vals = E2M1[nib]
    vals = vals * np.repeat(np.exp2(scales.astype(np.float64) - 127.0), 8, axis=1)[..., None]
    return vals.transpose(0, 1, 3, 2).reshape(g * 512, n)


def gelu(v):
    return 0.5 * v * (1.0 + np.tanh(np.sqrt(2.0 / np.pi) * (v + 0.044715 * v**3)))


K, T, S, H, P, N = 1024, 4096, 1024, 1024, 512, 512

def setup_inputs():
    n = np.random.standard_normal
    s = mx_kscale(K)[:, None]
    u = mx_kscale(H)[:, None]
    d = {}
    d["tab_words"], d["tab_scales"] = pack_weight(n((K, T)) * s, "e2m1")
    d["offs"] = striped(np.random.permutation(T)[:S])
    d["w1"] = (1.2 * n((K, H)) / s / K ** 0.5).astype(np.float32)
    d["b1"] = (0.6 * n(H)).astype(np.float32)
    d["w2_words"], d["w2_scales"] = pack_weight(0.8 * n((K, H)) / s / K ** 0.5, "e4m3")
    d["pos1"] = striped(np.random.permutation(S)[:P])
    d["pos2"] = striped(np.random.permutation(S)[:P])
    d["gain"] = (np.exp(0.3 * n(H)) * u[:, 0]).astype(np.float32)
    d["w3_words"], d["w3_scales"] = pack_weight(n((H, N)) / u / H ** 0.5, "e2m1")
    d["district"] = (0.8 * n((N, P))).astype(np.float32)
    return d

def reference(tab_words, tab_scales, offs, w1, b1, w2_words, w2_scales, pos1, pos2,
              gain, w3_words, w3_scales, district):
    v = unpack_weight(tab_words, tab_scales, "e2m1")[:, unstriped(offs)]
    w2 = unpack_weight(w2_words, w2_scales, "e4m3")
    w3 = unpack_weight(w3_words, w3_scales, "e2m1")
    h = (mxq(f64(w1), 0, "e4m3").T @ v) + f64(b1)[:, None]
    b = np.tanh(h) + (w2.T @ v)
    z = f64(gain)[:, None] * (h[:, unstriped(pos1)] * b[:, unstriped(pos2)])
    out = (w3.T @ mxq(z, 0, "e4m3")) + f64(district)
    return out

@@ -1,0 +1,255 @@
+from contextlib import ExitStack
+
+import concourse.mybir as mybir
+
+K, T, S, H, PAIRS, N = 1024, 4096, 1024, 1024, 512, 512
+FLOPS = 2 * K * H * S * 2 + 2 * H * N * PAIRS
+
+F32 = mybir.dt.float32
+BF16 = mybir.dt.bfloat16
+I32 = mybir.dt.int32
+U32 = mybir.dt.uint32
+U16 = mybir.dt.uint16
+U8 = mybir.dt.uint8
+FP8X4 = mybir.dt.float8_e4m3fn_x4
+FP4X4 = mybir.dt.float4_e2m1fn_x4
+ACT = mybir.ActivationFunctionType
+ALU = mybir.AluOpType
+
+P = 128
+PASS = 512
+BANK = 512
+
+
+def tile_list_duplicate_call_features_kernel(
+    tc, tab_words, tab_scales, offs, w1, b1, w2_words, w2_scales, pos1, pos2,
+    gain, w3_words, w3_scales, district, out,
+):
+    nc = tc.nc
+    with ExitStack() as ctx:
+        keep = ctx.enter_context(tc.tile_pool(name="keep", bufs=1))
+        ring = ctx.enter_context(tc.tile_pool(name="ring", bufs=3))
+        psum = ctx.enter_context(tc.psum_pool(name="psum", bufs=2))
+
+        def held(shape, dtype, name):
+            return keep.tile(shape, dtype, name=name, align_bytes=64)
+
+        offs_sb = held([P, S // 16], U16, "offs_sb")
+        pos1_sb = held([P, PAIRS // 16], U16, "pos1_sb")
+        pos2_sb = held([P, PAIRS // 16], U16, "pos2_sb")
+        tab_sc = held([P, T], U8, "tab_sc")
+        tab_w = [held([P, T], U16, "tab_w%d" % a) for a in range(2)]
+        v_w = [held([P, S], U16, "v_w%d" % a) for a in range(2)]
+        v_sc_all = held([P, S], U8, "v_sc_all")
+        v_sc = [held([P, S], U8, "v_sc%d" % a) for a in range(2)]
+        w1_raw = [[[held([P, 4, PASS // 2], F32, "w1_raw%d%d%d" % (b, a, u)) for u in range(2)]
+                   for a in range(2)] for b in range(2)]
+        w1_bf = [[held([P, 4 * PASS], BF16, "w1_bf%d%d" % (b, a)) for a in range(2)] for b in range(2)]
+        w1_w = [[held([P, PASS], U32, "w1_w%d%d" % (b, a)) for a in range(2)] for b in range(2)]
+        w1_sc = [[held([P, PASS], U8, "w1_sc%d%d" % (b, a)) for a in range(2)] for b in range(2)]
+        w2_raw = [held([P, 2, PASS], U32, "w2_raw%d" % b) for b in range(2)]
+        w2_w = [held([P, 2, PASS], U32, "w2_w%d" % b) for b in range(2)]
+        w2_sc_raw = held([P, 2, H], U8, "w2_sc_raw")
+        w2_sc = [held([P, 2, PASS], U8, "w2_sc%d" % b) for b in range(2)]
+        w3_w = held([P, 2, 2 * N], U8, "w3_w")
+        w3_sc = held([P, 2, N], U8, "w3_sc")
+        b1_sb = held([P, 2, 4], F32, "b1_sb")
+        gain_sb = held([P, 2, 4], F32, "gain_sb")
+        gb_sb = held([P, 2, 4], F32, "gb_sb")
+        dist_sb = held([P, 4, PAIRS], F32, "dist_sb")
+        z_f = [held([P, 4, PAIRS], F32, "z_f%d" % b) for b in range(2)]
+        z_bf = [held([P, 4 * PAIRS], BF16, "z_bf%d" % b) for b in range(2)]
+        z_w = [held([P, PAIRS], U32, "z_w%d" % b) for b in range(2)]
+        z_sc = [held([P, PAIRS], U8, "z_sc%d" % b) for b in range(2)]
+        warm = held([P, 1], F32, "warm")
+
+        for q in range(4):
+            eng = nc.vector if q else nc.gpsimd
+            eng.memset(tab_sc[32 * q : 32 * q + 24, :].bitcast(I32), 0)
+        nc.gpsimd.memset(w2_sc_raw[:].rearrange("p a c -> p (a c)").bitcast(I32), 0)
+        for a in range(2):
+            nc.gpsimd.memset(v_sc[a][:].bitcast(I32), 0)
+        nc.gpsimd.memset(w3_sc[:].rearrange("p a c -> p (a c)").bitcast(I32), 0)
+        nc.vector.memset(warm[:], 0.0)
+        nc.scalar.activation(out=warm[:], in_=warm[:], func=ACT.Tanh)
+
+        def load_w1(b, a):
+            for u in range(2):
+                c0 = PASS * b + 256 * u
+                src = w1[PASS * a : PASS * (a + 1), c0 : c0 + 256]
+                nc.sync.dma_start(out=w1_raw[b][a][u][:], in_=src.rearrange("(p j) c -> p j c", j=4))
+
+        def load_w2(b):
+            src = w2_words.rearrange("a p c i -> p a (c i)")[:, :, 4 * PASS * b : 4 * PASS * (b + 1)]
+            nc.sync.dma_start(out=w2_raw[b][:].bitcast(I32), in_=src.bitcast(I32))
+
+        def load_planes(dst, src):
+            for q in range(4):
+                nc.sync.dma_start(
+                    out=dst[32 * q : 32 * q + 4, :, :].bitcast(I32),
+                    in_=src[:, 4 * q : 4 * q + 4, :].rearrange("a r c -> r a c").bitcast(I32),
+                )
+
+        nc.sync.dma_start(offs_sb[:], offs)
+        for q in range(4):
+            nc.sync.dma_start(
+                out=tab_sc[32 * q + 24 : 32 * q + 32, :].bitcast(I32),
+                in_=tab_scales[:, 4 * q : 4 * q + 4, :].bitcast(I32),
+            )
+        nc.sync.dma_start(out=tab_w[0][:].bitcast(I32), in_=tab_words[0].bitcast(I32))
+        load_w1(0, 0)
+        nc.sync.dma_start(out=tab_w[1][:].bitcast(I32), in_=tab_words[1].bitcast(I32))
+        load_w1(0, 1)
+        load_planes(w2_sc_raw, w2_scales)
+        load_w2(0)
+        nc.sync.dma_start(out=b1_sb[:], in_=b1.rearrange("(b p t) -> p b t", b=2, t=4))
+        nc.sync.dma_start(out=gain_sb[:], in_=gain.rearrange("(b p t) -> p b t", b=2, t=4))
+        nc.sync.dma_start(pos1_sb[:], pos1)
+        nc.sync.dma_start(pos2_sb[:], pos2)
+
+        def cast_w1(b, a, u, engine):
+            dst = w1_bf[b][a][:].rearrange("p (t m j) -> p m j t", t=4, j=4)[:, 64 * u : 64 * (u + 1)]
+            src = w1_raw[b][a][u][:].rearrange("p j (m t) -> p m j t", t=4)
+            if engine == "scalar":
+                nc.scalar.activation(out=dst, in_=src, func=ACT.Copy)
+            else:
+                nc.vector.tensor_copy(out=dst, in_=src)
+
+        def quant_w1(b, a, t0, t1):
+            nc.vector.quantize_mx(out=w1_w[b][a][:, P * t0 : P * t1].bitcast(FP8X4), scales=w1_sc[b][a][:, P * t0 : P * t1],
+                                  in_=w1_bf[b][a][:, 4 * P * t0 : 4 * P * t1])
+
+        def deal_w2_words(b):
+            nc.vector.tensor_copy(
+                out=w2_w[b][:].rearrange("p a (t c i) -> p a c t i", t=4, i=4),
+                in_=w2_raw[b][:].rearrange("p a (c i t) -> p a c t i", t=4, i=4),
+            )
+
+        def deal_w2_scales(b):
+            nc.vector.tensor_copy(
+                out=w2_sc[b][:].rearrange("p a (t m) -> p a t m", t=4),
+                in_=w2_sc_raw[:, :, PASS * b : PASS * (b + 1)].rearrange("p a (m t) -> p a t m", t=4),
+            )
+
+        nc.vector.tensor_copy(v_sc_all[:], tab_sc[:].indirect(offs_sb[:]))
+        for a in range(2):
+            shift = 24 + 4 * a
+            nc.scalar.dma_start(out=v_sc[a][0:100, :].bitcast(I32), in_=v_sc_all[shift : shift + 100, :].bitcast(I32))
+        nc.vector.tensor_copy(v_w[0][:], tab_w[0][:].indirect(offs_sb[:]))
+        cast_w1(0, 0, 0, "scalar")
+        cast_w1(0, 0, 1, "scalar")
+        nc.vector.tensor_copy(v_w[1][:], tab_w[1][:].indirect(offs_sb[:]))
+        quant_w1(0, 0, 0, 4)
+        cast_w1(0, 1, 0, "scalar")
+        cast_w1(0, 1, 1, "vector")
+        deal_w2_scales(0)
+        quant_w1(0, 1, 0, 2)
+        deal_w2_words(0)
+        quant_w1(0, 1, 2, 4)
+        nc.vector.tensor_tensor(gb_sb[:], gain_sb[:], b1_sb[:], ALU.mult)
+
+        load_w1(1, 0)
+        load_w1(1, 1)
+        load_w2(1)
+        load_planes(w3_sc, w3_scales)
+        nc.sync.dma_start(out=w3_w[:].bitcast(I32), in_=w3_words.rearrange("a p c -> p a c").bitcast(I32))
+        nc.sync.dma_start(out=dist_sb[:], in_=district.rearrange("(c p) m -> p c m", p=P))
+
+        def product(tag, words, scales, half):
+            acc = psum.tile([P, BANK], F32, name=tag, tag=tag)
+            for a in range(2):
+                nc.tensor.matmul_mx(
+                    out=acc[:], lhsT=words[a].bitcast(FP8X4), lhsT_scale=scales[a],
+                    rhs=v_w[a][:, BANK * half : BANK * (half + 1)].bitcast(FP4X4),
+                    rhs_scale=v_sc[a][:, BANK * half : BANK * (half + 1)],
+                    start=(a == 0), stop=(a == 1),
+                )
+            return acc
+
+        def first_stage(s):
+            b, t = divmod(s, 4)
+            cols = slice(P * t, P * (t + 1))
+            acc1 = [product("acc1_%d" % half, [w1_w[b][a][:, cols] for a in range(2)],
+                            [w1_sc[b][a][:, cols] for a in range(2)], half) for half in range(2)]
+            acc2 = [product("acc2_%d" % half, [w2_w[b][:, a, cols] for a in range(2)],
+                            [w2_sc[b][:, a, cols] for a in range(2)], half) for half in range(2)]
+            gh = ring.tile([P, S], F32, name="gh")
+            th = ring.tile([P, S], F32, name="th")
+            bb = ring.tile([P, S], F32, name="bb")
+            for half in range(2):
+                cs = slice(BANK * half, BANK * (half + 1))
+                nc.scalar.activation(out=gh[:, cs], in_=acc1[half][:], func=ACT.Identity,
+                                     bias=gb_sb[:, b, t : t + 1], scale=gain_sb[:, b, t : t + 1])
+                nc.scalar.activation(out=th[:, cs], in_=acc1[half][:], func=ACT.Tanh, bias=b1_sb[:, b, t : t + 1])
+            for half in range(2):
+                cs = slice(BANK * half, BANK * (half + 1))
+                nc.vector.tensor_tensor(bb[:, cs], acc2[half][:], th[:, cs], ALU.add)
+            early = ring.tile([P, PAIRS], F32, name="early")
+            nc.vector.tensor_copy(early[:], gh[:].indirect(pos1_sb[:]))
+            return bb, early
+
+        def pair_product(s, bb, early, m0=0, m1=PAIRS):
+            b, t = divmod(s, 4)
+            nc.vector.tensor_tensor(z_f[b][:, t, m0:m1], bb[:].indirect(pos2_sb[:, m0 // 16 : m1 // 16]),
+                                    early[:, m0:m1], ALU.mult)
+
+        def weave_z(b, c0, c1, engine):
+            dst = z_bf[b][:].rearrange("p (c i t) -> p c t i", i=4, t=4)[:, c0:c1]
+            src = z_f[b][:].rearrange("p t (c i) -> p c t i", i=4)[:, c0:c1]
+            if engine == "scalar":
+                nc.scalar.activation(out=dst, in_=src, func=ACT.Copy)
+            else:
+                nc.vector.tensor_copy(out=dst, in_=src)
+
+        def quant_z(b, m0=0, m1=PAIRS):
+            nc.vector.quantize_mx(out=z_w[b][:, m0:m1].bitcast(FP8X4), scales=z_sc[b][:, m0:m1],
+                                  in_=z_bf[b][:, 4 * m0 : 4 * m1])
+
+        pending = None
+        for s in range(8):
+            made = first_stage(s)
+            if pending is not None:
+                pair_product(s - 1, *pending)
+            pending = made
+            if s < 4:
+                cast_w1(1, s // 2, s % 2, "scalar")
+            if s == 0:
+                deal_w2_scales(1)
+            if s == 1:
+                deal_w2_words(1)
+            if s in (2, 3):
+                quant_w1(1, s - 2, 0, 4)
+            if s in (4, 5):
+                weave_z(0, 64 * (s - 4), 64 * (s - 3), "scalar")
+            if s == 6:
+                quant_z(0)
+        tags = ["acc1_0", "acc1_1", "acc2_0", "acc2_1"]
+        feats = [psum.tile([P, 4, P], F32, name=tags[u], tag=tags[u]) for u in range(4)]
+        out_v = out.rearrange("(c p) m -> p c m", p=P)
+
+        def last_pass(b, u):
+            for c in range(4):
+                nc.tensor.matmul_mx(
+                    out=feats[u][:, c, :], lhsT=w3_w[:, b, 2 * P * c : 2 * P * (c + 1)].bitcast(FP4X4),
+                    lhsT_scale=w3_sc[:, b, P * c : P * (c + 1)],
+                    rhs=z_w[b][:, P * u : P * (u + 1)].bitcast(FP8X4), rhs_scale=z_sc[b][:, P * u : P * (u + 1)],
+                    start=(b == 0 and c == 0), stop=(b == 1 and c == 3),
+                )
+
+        def finish(u):
+            res = ring.tile([P, 4, P], F32, name="res", bufs=4)
+            nc.vector.tensor_tensor(res[:], feats[u][:], dist_sb[:, :, P * u : P * (u + 1)], ALU.add)
+            nc.sync.dma_start(out=out_v[:, :, P * u : P * (u + 1)], in_=res[:])
+
+        for u in range(4):
+            last_pass(0, u)
+        for step in range(7):
+            if step < 4:
+                pair_product(7, *pending, P * step, P * (step + 1))
+                weave_z(1, 32 * step, 32 * (step + 1), "scalar")
+            if 1 <= step < 5:
+                u = step - 1
+                quant_z(1, P * u, P * (u + 1))
+                last_pass(1, u)
+            if step >= 3:
+                finish(step - 3)

@@ -31,8 +31,8 @@ def tile_list_duplicate_call_features_kernel(
         ring = ctx.enter_context(tc.tile_pool(name="ring", bufs=3))
         psum = ctx.enter_context(tc.psum_pool(name="psum", bufs=2))
 
-        def held(shape, dtype, name):
-            return keep.tile(shape, dtype, name=name, align_bytes=64)
+        def held(shape, dtype, name, tag=""):
+            return keep.tile(shape, dtype, name=name, tag=tag or name, align_bytes=64)
 
         offs_sb = held([P, S // 16], U16, "offs_sb")
         pos1_sb = held([P, PAIRS // 16], U16, "pos1_sb")
@@ -40,76 +40,62 @@ def tile_list_duplicate_call_features_kernel(
         tab_sc = held([P, T], U8, "tab_sc")
         tab_w = [held([P, T], U16, "tab_w%d" % a) for a in range(2)]
         v_w = [held([P, S], U16, "v_w%d" % a) for a in range(2)]
-        v_sc_all = held([P, S], U8, "v_sc_all")
         v_sc = [held([P, S], U8, "v_sc%d" % a) for a in range(2)]
-        w1_raw = [[[held([P, 4, PASS // 2], F32, "w1_raw%d%d%d" % (b, a, u)) for u in range(2)]
-                   for a in range(2)] for b in range(2)]
+        w1_raw, w2_raw = {}, {}
         w1_bf = [[held([P, 4 * PASS], BF16, "w1_bf%d%d" % (b, a)) for a in range(2)] for b in range(2)]
         w1_w = [[held([P, PASS], U32, "w1_w%d%d" % (b, a)) for a in range(2)] for b in range(2)]
         w1_sc = [[held([P, PASS], U8, "w1_sc%d%d" % (b, a)) for a in range(2)] for b in range(2)]
-        w2_raw = [held([P, 2, PASS], U32, "w2_raw%d" % b) for b in range(2)]
         w2_w = [held([P, 2, PASS], U32, "w2_w%d" % b) for b in range(2)]
         w2_sc_raw = held([P, 2, H], U8, "w2_sc_raw")
         w2_sc = [held([P, 2, PASS], U8, "w2_sc%d" % b) for b in range(2)]
-        w3_w = held([P, 2, 2 * N], U8, "w3_w")
-        w3_sc = held([P, 2, N], U8, "w3_sc")
         b1_sb = held([P, 2, 4], F32, "b1_sb")
         gain_sb = held([P, 2, 4], F32, "gain_sb")
         gb_sb = held([P, 2, 4], F32, "gb_sb")
-        dist_sb = held([P, 4, PAIRS], F32, "dist_sb")
         z_f = [held([P, 4, PAIRS], F32, "z_f%d" % b) for b in range(2)]
         z_bf = [held([P, 4 * PAIRS], BF16, "z_bf%d" % b) for b in range(2)]
         z_w = [held([P, PAIRS], U32, "z_w%d" % b) for b in range(2)]
         z_sc = [held([P, PAIRS], U8, "z_sc%d" % b) for b in range(2)]
         warm = held([P, 1], F32, "warm")
 
-        for q in range(4):
-            eng = nc.vector if q else nc.gpsimd
-            eng.memset(tab_sc[32 * q : 32 * q + 24, :].bitcast(I32), 0)
-        nc.gpsimd.memset(w2_sc_raw[:].rearrange("p a c -> p (a c)").bitcast(I32), 0)
-        for a in range(2):
-            nc.gpsimd.memset(v_sc[a][:].bitcast(I32), 0)
-        nc.gpsimd.memset(w3_sc[:].rearrange("p a c -> p (a c)").bitcast(I32), 0)
+        nc.vector.memset(tab_sc[:].bitcast(I32), 0)
+        nc.vector.memset(w2_sc_raw[:].rearrange("p a c -> p (a c)").bitcast(I32), 0)
+        nc.vector.memset(v_sc[1][:].bitcast(I32), 0)
         nc.vector.memset(warm[:], 0.0)
         nc.scalar.activation(out=warm[:], in_=warm[:], func=ACT.Tanh)
 
         def load_w1(b, a):
-            for u in range(2):
-                c0 = PASS * b + 256 * u
-                src = w1[PASS * a : PASS * (a + 1), c0 : c0 + 256]
-                nc.sync.dma_start(out=w1_raw[b][a][u][:], in_=src.rearrange("(p j) c -> p j c", j=4))
+            src = w1[PASS * a : PASS * (a + 1), PASS * b : PASS * (b + 1)]
+            w1_raw[b, a] = held([P, 4, PASS], F32, "w1_raw%d%d" % (b, a), "w1_raw%d" % a)
+            nc.sync.dma_start(out=w1_raw[b, a][:], in_=src.rearrange("(p j) c -> p j c", j=4))
 
         def load_w2(b):
             src = w2_words.rearrange("a p c i -> p a (c i)")[:, :, 4 * PASS * b : 4 * PASS * (b + 1)]
+            w2_raw[b] = held([P, 2, PASS], U32, "w2_raw%d" % b, "tab_sc")
             nc.sync.dma_start(out=w2_raw[b][:].bitcast(I32), in_=src.bitcast(I32))
 
-        def load_planes(dst, src):
+        def load_planes(dst, src, queue):
             for q in range(4):
-                nc.sync.dma_start(
+                queue.dma_start(
                     out=dst[32 * q : 32 * q + 4, :, :].bitcast(I32),
                     in_=src[:, 4 * q : 4 * q + 4, :].rearrange("a r c -> r a c").bitcast(I32),
                 )
 
         nc.sync.dma_start(offs_sb[:], offs)
-        for q in range(4):
-            nc.sync.dma_start(
-                out=tab_sc[32 * q + 24 : 32 * q + 32, :].bitcast(I32),
-                in_=tab_scales[:, 4 * q : 4 * q + 4, :].bitcast(I32),
-            )
         nc.sync.dma_start(out=tab_w[0][:].bitcast(I32), in_=tab_words[0].bitcast(I32))
+        nc.sync.dma_start(out=tab_sc[4:P:8, :].bitcast(I32), in_=tab_scales[1].bitcast(I32))
+        for q in range(4):
+            nc.sync.dma_start(out=tab_sc[32 * q : 32 * q + 4, :].bitcast(I32),
+                              in_=tab_scales[0, 4 * q : 4 * q + 4, :].bitcast(I32))
         load_w1(0, 0)
         nc.sync.dma_start(out=tab_w[1][:].bitcast(I32), in_=tab_words[1].bitcast(I32))
         load_w1(0, 1)
-        load_planes(w2_sc_raw, w2_scales)
-        load_w2(0)
-        nc.sync.dma_start(out=b1_sb[:], in_=b1.rearrange("(b p t) -> p b t", b=2, t=4))
-        nc.sync.dma_start(out=gain_sb[:], in_=gain.rearrange("(b p t) -> p b t", b=2, t=4))
-        nc.sync.dma_start(pos1_sb[:], pos1)
-        nc.sync.dma_start(pos2_sb[:], pos2)
+        nc.gpsimd.dma_start(out=b1_sb[:], in_=b1.rearrange("(b p t) -> p b t", b=2, t=4))
+        nc.gpsimd.dma_start(out=gain_sb[:], in_=gain.rearrange("(b p t) -> p b t", b=2, t=4))
+        load_planes(w2_sc_raw, w2_scales, nc.gpsimd)
 
-        def cast_w1(b, a, u, engine):
-            dst = w1_bf[b][a][:].rearrange("p (t m j) -> p m j t", t=4, j=4)[:, 64 * u : 64 * (u + 1)]
-            src = w1_raw[b][a][u][:].rearrange("p j (m t) -> p m j t", t=4)
+        def cast_w1(b, a, m0, m1, engine):
+            dst = w1_bf[b][a][:].rearrange("p (t m j) -> p m j t", t=4, j=4)[:, m0:m1]
+            src = w1_raw[b, a][:].rearrange("p j (m t) -> p m j t", t=4)[:, m0:m1]
             if engine == "scalar":
                 nc.scalar.activation(out=dst, in_=src, func=ACT.Copy)
             else:
@@ -131,18 +117,19 @@ def tile_list_duplicate_call_features_kernel(
                 in_=w2_sc_raw[:, :, PASS * b : PASS * (b + 1)].rearrange("p a (m t) -> p a t m", t=4),
             )
 
-        nc.vector.tensor_copy(v_sc_all[:], tab_sc[:].indirect(offs_sb[:]))
-        for a in range(2):
-            shift = 24 + 4 * a
-            nc.scalar.dma_start(out=v_sc[a][0:100, :].bitcast(I32), in_=v_sc_all[shift : shift + 100, :].bitcast(I32))
         nc.vector.tensor_copy(v_w[0][:], tab_w[0][:].indirect(offs_sb[:]))
-        cast_w1(0, 0, 0, "scalar")
-        cast_w1(0, 0, 1, "scalar")
+        nc.vector.tensor_copy(v_sc[0][:], tab_sc[:].indirect(offs_sb[:]))
+        for r in range(4):
+            nc.sync.dma_start(out=v_sc[1][r:P:32, :].bitcast(I32), in_=v_sc[0][8 * r + 4 : P : 32, :].bitcast(I32))
+        load_w2(0)
+        nc.sync.dma_start(pos1_sb[:], pos1)
+        nc.sync.dma_start(pos2_sb[:], pos2)
+        cast_w1(0, 0, 0, P, "scalar")
+        deal_w2_scales(0)
         nc.vector.tensor_copy(v_w[1][:], tab_w[1][:].indirect(offs_sb[:]))
         quant_w1(0, 0, 0, 4)
-        cast_w1(0, 1, 0, "scalar")
-        cast_w1(0, 1, 1, "vector")
-        deal_w2_scales(0)
+        cast_w1(0, 1, 0, 48, "scalar")
+        cast_w1(0, 1, 48, P, "vector")
         quant_w1(0, 1, 0, 2)
         deal_w2_words(0)
         quant_w1(0, 1, 2, 4)
@@ -151,8 +138,12 @@ def tile_list_duplicate_call_features_kernel(
         load_w1(1, 0)
         load_w1(1, 1)
         load_w2(1)
-        load_planes(w3_sc, w3_scales)
+        w3_w = held([P, 2, 2 * N], U8, "w3_w", "tab_w1")
         nc.sync.dma_start(out=w3_w[:].bitcast(I32), in_=w3_words.rearrange("a p c -> p a c").bitcast(I32))
+        w3_sc = held([P, 2, N], U8, "w3_sc", "w1_bf00")
+        nc.vector.memset(w3_sc[:].rearrange("p a c -> p (a c)").bitcast(I32), 0)
+        load_planes(w3_sc, w3_scales, nc.sync)
+        dist_sb = held([P, 4, PAIRS], F32, "dist_sb", "w1_bf01")
         nc.sync.dma_start(out=dist_sb[:], in_=district.rearrange("(c p) m -> p c m", p=P))
 
         def product(tag, words, scales, half):
@@ -193,6 +184,12 @@ def tile_list_duplicate_call_features_kernel(
             nc.vector.tensor_tensor(z_f[b][:, t, m0:m1], bb[:].indirect(pos2_sb[:, m0 // 16 : m1 // 16]),
                                     early[:, m0:m1], ALU.mult)
 
+        def pair_product_apart(s, bb, early):
+            b, t = divmod(s, 4)
+            late = ring.tile([P, PAIRS], F32, name="late")
+            nc.vector.tensor_copy(late[:], bb[:].indirect(pos2_sb[:]))
+            nc.gpsimd.tensor_tensor(z_f[b][:, t, :], late[:], early[:], ALU.mult)
+
         def weave_z(b, c0, c1, engine):
             dst = z_bf[b][:].rearrange("p (c i t) -> p c t i", i=4, t=4)[:, c0:c1]
             src = z_f[b][:].rearrange("p t (c i) -> p c t i", i=4)[:, c0:c1]
@@ -209,10 +206,10 @@ def tile_list_duplicate_call_features_kernel(
         for s in range(8):
             made = first_stage(s)
             if pending is not None:
-                pair_product(s - 1, *pending)
+                pair_product_apart(s - 1, *pending)
             pending = made
             if s < 4:
-                cast_w1(1, s // 2, s % 2, "scalar")
+                cast_w1(1, s // 2, 64 * (s % 2), 64 * (s % 2 + 1), "scalar")
             if s == 0:
                 deal_w2_scales(1)
             if s == 1:

@@ -38,16 +38,13 @@ def tile_list_duplicate_call_features_kernel(
         pos1_sb = held([P, PAIRS // 16], U16, "pos1_sb")
         pos2_sb = held([P, PAIRS // 16], U16, "pos2_sb")
         tab_sc = held([P, T], U8, "tab_sc")
-        tab_w = [held([P, T], U16, "tab_w%d" % a) for a in range(2)]
         v_w = [held([P, S], U16, "v_w%d" % a) for a in range(2)]
         v_sc = [held([P, S], U8, "v_sc%d" % a) for a in range(2)]
-        w1_raw, w2_raw = {}, {}
+        w1_raw, w2_raw, w2_w, w2_sc = {}, {}, {}, {}
         w1_bf = [[held([P, 4 * PASS], BF16, "w1_bf%d%d" % (b, a)) for a in range(2)] for b in range(2)]
         w1_w = [[held([P, PASS], U32, "w1_w%d%d" % (b, a)) for a in range(2)] for b in range(2)]
         w1_sc = [[held([P, PASS], U8, "w1_sc%d%d" % (b, a)) for a in range(2)] for b in range(2)]
-        w2_w = [held([P, 2, PASS], U32, "w2_w%d" % b) for b in range(2)]
         w2_sc_raw = held([P, 2, H], U8, "w2_sc_raw")
-        w2_sc = [held([P, 2, PASS], U8, "w2_sc%d" % b) for b in range(2)]
         b1_sb = held([P, 2, 4], F32, "b1_sb")
         gain_sb = held([P, 2, 4], F32, "gain_sb")
         gb_sb = held([P, 2, 4], F32, "gb_sb")
@@ -55,17 +52,20 @@ def tile_list_duplicate_call_features_kernel(
         z_bf = [held([P, 4 * PAIRS], BF16, "z_bf%d" % b) for b in range(2)]
         z_w = [held([P, PAIRS], U32, "z_w%d" % b) for b in range(2)]
         z_sc = [held([P, PAIRS], U8, "z_sc%d" % b) for b in range(2)]
-        warm = held([P, 1], F32, "warm")
+        warm = held([P, 1], F32, "warm", "tab_w1")
+        warm_out = held([P, 1], F32, "warm_out", "w1_raw0")
 
-        nc.vector.memset(tab_sc[:].bitcast(I32), 0)
+        nc.gpsimd.memset(tab_sc[:].bitcast(I32), 0)
         nc.vector.memset(w2_sc_raw[:].rearrange("p a c -> p (a c)").bitcast(I32), 0)
         nc.vector.memset(v_sc[1][:].bitcast(I32), 0)
         nc.vector.memset(warm[:], 0.0)
-        nc.scalar.activation(out=warm[:], in_=warm[:], func=ACT.Tanh)
+        nc.scalar.activation(out=warm_out[:], in_=warm[:], func=ACT.Tanh)
+
+        tab_w = [held([P, T], U16, "tab_w%d" % a) for a in range(2)]
 
         def load_w1(b, a):
             src = w1[PASS * a : PASS * (a + 1), PASS * b : PASS * (b + 1)]
-            w1_raw[b, a] = held([P, 4, PASS], F32, "w1_raw%d%d" % (b, a), "w1_raw%d" % a)
+            w1_raw[b, a] = held([P, 4, PASS], F32, "w1_raw%d%d" % (b, a), ("w1_raw0", "tab_w0")[a])
             nc.sync.dma_start(out=w1_raw[b, a][:], in_=src.rearrange("(p j) c -> p j c", j=4))
 
         def load_w2(b):
@@ -81,17 +81,18 @@ def tile_list_duplicate_call_features_kernel(
                 )
 
         nc.sync.dma_start(offs_sb[:], offs)
+        nc.sync.dma_start(pos1_sb[:], pos1)
+        nc.sync.dma_start(pos2_sb[:], pos2)
         nc.sync.dma_start(out=tab_w[0][:].bitcast(I32), in_=tab_words[0].bitcast(I32))
-        nc.sync.dma_start(out=tab_sc[4:P:8, :].bitcast(I32), in_=tab_scales[1].bitcast(I32))
+        nc.sync.dma_start(out=tab_sc[8:24, :].bitcast(I32), in_=tab_scales[1].bitcast(I32))
         for q in range(4):
             nc.sync.dma_start(out=tab_sc[32 * q : 32 * q + 4, :].bitcast(I32),
                               in_=tab_scales[0, 4 * q : 4 * q + 4, :].bitcast(I32))
-        load_w1(0, 0)
         nc.sync.dma_start(out=tab_w[1][:].bitcast(I32), in_=tab_words[1].bitcast(I32))
-        load_w1(0, 1)
+        load_w1(0, 0)
+        load_planes(w2_sc_raw, w2_scales, nc.gpsimd)
         nc.gpsimd.dma_start(out=b1_sb[:], in_=b1.rearrange("(b p t) -> p b t", b=2, t=4))
         nc.gpsimd.dma_start(out=gain_sb[:], in_=gain.rearrange("(b p t) -> p b t", b=2, t=4))
-        load_planes(w2_sc_raw, w2_scales, nc.gpsimd)
 
         def cast_w1(b, a, m0, m1, engine):
             dst = w1_bf[b][a][:].rearrange("p (t m j) -> p m j t", t=4, j=4)[:, m0:m1]
@@ -106,45 +107,43 @@ def tile_list_duplicate_call_features_kernel(
                                   in_=w1_bf[b][a][:, 4 * P * t0 : 4 * P * t1])
 
         def deal_w2_words(b):
+            w2_w[b] = held([P, 2, PASS], U32, "w2_w%d" % b, ("w1_bf00", "w2_w1")[b])
             nc.vector.tensor_copy(
                 out=w2_w[b][:].rearrange("p a (t c i) -> p a c t i", t=4, i=4),
                 in_=w2_raw[b][:].rearrange("p a (c i t) -> p a c t i", t=4, i=4),
             )
 
         def deal_w2_scales(b):
+            w2_sc[b] = held([P, 2, PASS], U8, "w2_sc%d" % b, ("tab_w1", "w1_bf01")[b])
             nc.vector.tensor_copy(
                 out=w2_sc[b][:].rearrange("p a (t m) -> p a t m", t=4),
                 in_=w2_sc_raw[:, :, PASS * b : PASS * (b + 1)].rearrange("p a (m t) -> p a t m", t=4),
             )
 
         nc.vector.tensor_copy(v_w[0][:], tab_w[0][:].indirect(offs_sb[:]))
+        load_w1(0, 1)
         nc.vector.tensor_copy(v_sc[0][:], tab_sc[:].indirect(offs_sb[:]))
-        for r in range(4):
-            nc.sync.dma_start(out=v_sc[1][r:P:32, :].bitcast(I32), in_=v_sc[0][8 * r + 4 : P : 32, :].bitcast(I32))
+        for q in range(4):
+            nc.sync.dma_start(out=v_sc[1][32 * q : 32 * q + 4, :].bitcast(I32),
+                              in_=v_sc[0][8 + 4 * q : 12 + 4 * q, :].bitcast(I32))
         load_w2(0)
-        nc.sync.dma_start(pos1_sb[:], pos1)
-        nc.sync.dma_start(pos2_sb[:], pos2)
         cast_w1(0, 0, 0, P, "scalar")
-        deal_w2_scales(0)
         nc.vector.tensor_copy(v_w[1][:], tab_w[1][:].indirect(offs_sb[:]))
-        quant_w1(0, 0, 0, 4)
-        cast_w1(0, 1, 0, 48, "scalar")
-        cast_w1(0, 1, 48, P, "vector")
-        quant_w1(0, 1, 0, 2)
+        deal_w2_scales(0)
+        cast_w1(0, 1, 0, 40, "scalar")
+        cast_w1(0, 1, 40, P, "vector")
+        quant_w1(0, 0, 0, 1)
+        quant_w1(0, 1, 0, 1)
+        quant_w1(0, 0, 1, 2)
+        quant_w1(0, 0, 2, 4)
         deal_w2_words(0)
+        quant_w1(0, 1, 1, 2)
         quant_w1(0, 1, 2, 4)
-        nc.vector.tensor_tensor(gb_sb[:], gain_sb[:], b1_sb[:], ALU.mult)
+        nc.gpsimd.tensor_tensor(gb_sb[:], gain_sb[:], b1_sb[:], ALU.mult)
 
         load_w1(1, 0)
         load_w1(1, 1)
         load_w2(1)
-        w3_w = held([P, 2, 2 * N], U8, "w3_w", "tab_w1")
-        nc.sync.dma_start(out=w3_w[:].bitcast(I32), in_=w3_words.rearrange("a p c -> p a c").bitcast(I32))
-        w3_sc = held([P, 2, N], U8, "w3_sc", "w1_bf00")
-        nc.vector.memset(w3_sc[:].rearrange("p a c -> p (a c)").bitcast(I32), 0)
-        load_planes(w3_sc, w3_scales, nc.sync)
-        dist_sb = held([P, 4, PAIRS], F32, "dist_sb", "w1_bf01")
-        nc.sync.dma_start(out=dist_sb[:], in_=district.rearrange("(c p) m -> p c m", p=P))
 
         def product(tag, words, scales, half):
             acc = psum.tile([P, BANK], F32, name=tag, tag=tag)
@@ -216,6 +215,14 @@ def tile_list_duplicate_call_features_kernel(
                 deal_w2_words(1)
             if s in (2, 3):
                 quant_w1(1, s - 2, 0, 4)
+            if s == 3:
+                w3_w = held([P, 2, 2 * N], U8, "w3_w", "w1_bf10")
+                nc.sync.dma_start(out=w3_w[:].bitcast(I32), in_=w3_words.rearrange("a p c -> p a c").bitcast(I32))
+                w3_sc = held([P, 2, N], U8, "w3_sc", "w1_bf11")
+                nc.vector.memset(w3_sc[:].rearrange("p a c -> p (a c)").bitcast(I32), 0)
+                load_planes(w3_sc, w3_scales, nc.sync)
+                dist_sb = held([P, 4, PAIRS], F32, "dist_sb", "w1_raw0")
+                nc.sync.dma_start(out=dist_sb[:], in_=district.rearrange("(c p) m -> p c m", p=P))
             if s in (4, 5):
                 weave_z(0, 64 * (s - 4), 64 * (s - 3), "scalar")
             if s == 6:

@@ -163,20 +163,21 @@ def tile_list_duplicate_call_features_kernel(
                             [w1_sc[b][a][:, cols] for a in range(2)], half) for half in range(2)]
             acc2 = [product("acc2_%d" % half, [w2_w[b][:, a, cols] for a in range(2)],
                             [w2_sc[b][:, a, cols] for a in range(2)], half) for half in range(2)]
-            gh = ring.tile([P, S], F32, name="gh")
+            rows = ring.tile([P, 2 * S], F32, name="rows")
             th = ring.tile([P, S], F32, name="th")
-            bb = ring.tile([P, S], F32, name="bb")
             for half in range(2):
                 cs = slice(BANK * half, BANK * (half + 1))
-                nc.scalar.activation(out=gh[:, cs], in_=acc1[half][:], func=ACT.Identity,
-                                     bias=gb_sb[:, b, t : t + 1], scale=gain_sb[:, b, t : t + 1])
                 nc.scalar.activation(out=th[:, cs], in_=acc1[half][:], func=ACT.Tanh, bias=b1_sb[:, b, t : t + 1])
             for half in range(2):
+                cs = slice(S + BANK * half, S + BANK * (half + 1))
+                nc.scalar.activation(out=rows[:, cs], in_=acc1[half][:], func=ACT.Identity,
+                                     bias=gb_sb[:, b, t : t + 1], scale=gain_sb[:, b, t : t + 1])
+            for half in range(2):
                 cs = slice(BANK * half, BANK * (half + 1))
-                nc.vector.tensor_tensor(bb[:, cs], acc2[half][:], th[:, cs], ALU.add)
+                nc.vector.tensor_tensor(rows[:, cs], acc2[half][:], th[:, cs], ALU.add)
             early = ring.tile([P, PAIRS], F32, name="early")
-            nc.vector.tensor_copy(early[:], gh[:].indirect(pos1_sb[:]))
-            return bb, early
+            nc.vector.tensor_copy(early[:], rows[:, S : 2 * S].indirect(pos1_sb[:]))
+            return rows, early
 
         def pair_product(s, bb, early, m0=0, m1=PAIRS):
             b, t = divmod(s, 4)
@@ -201,12 +202,10 @@ def tile_list_duplicate_call_features_kernel(
             nc.vector.quantize_mx(out=z_w[b][:, m0:m1].bitcast(FP8X4), scales=z_sc[b][:, m0:m1],
                                   in_=z_bf[b][:, 4 * m0 : 4 * m1])
 
-        pending = None
         for s in range(8):
-            made = first_stage(s)
-            if pending is not None:
-                pair_product_apart(s - 1, *pending)
-            pending = made
+            pending = first_stage(s)
+            if s < 7:
+                pair_product_apart(s, *pending)
             if s < 4:
                 cast_w1(1, s // 2, 64 * (s % 2), 64 * (s % 2 + 1), "scalar")
             if s == 0:

@@ -3,7 +3,7 @@ from contextlib import ExitStack
 import concourse.mybir as mybir
 
 K, T, S, H, PAIRS, N = 1024, 4096, 1024, 1024, 512, 512
-FLOPS = 2 * K * H * S * 2 + 2 * H * N * PAIRS
+FLOPS = 2 * (2 * K * H * S) + 2 * H * N * PAIRS
 
 F32 = mybir.dt.float32
 BF16 = mybir.dt.bfloat16
@@ -17,8 +17,18 @@ ACT = mybir.ActivationFunctionType
 ALU = mybir.AluOpType
 
 P = 128
-PASS = 512
+PACK = 4
+PASS = P * PACK
+K_PASSES = K // PASS
+R_PASSES = H // PASS
+SLICES = R_PASSES * PACK
+QUADS = 4
 BANK = 512
+LIST_COL = 16
+SPARE_ROW = 8
+CHUNK = 128
+CHUNKS = PAIRS // CHUNK
+RING = 3
 
 
 def tile_list_duplicate_call_features_kernel(
@@ -28,53 +38,53 @@ def tile_list_duplicate_call_features_kernel(
     nc = tc.nc
     with ExitStack() as ctx:
         keep = ctx.enter_context(tc.tile_pool(name="keep", bufs=1))
-        ring = ctx.enter_context(tc.tile_pool(name="ring", bufs=3))
+        ring = ctx.enter_context(tc.tile_pool(name="ring", bufs=RING))
         psum = ctx.enter_context(tc.psum_pool(name="psum", bufs=2))
 
-        def held(shape, dtype, name, tag=""):
-            return keep.tile(shape, dtype, name=name, tag=tag or name, align_bytes=64)
+        def held(shape, dtype, name, on_bytes_of=""):
+            return keep.tile(shape, dtype, name=name, tag=on_bytes_of or name, align_bytes=64)
 
-        offs_sb = held([P, S // 16], U16, "offs_sb")
-        pos1_sb = held([P, PAIRS // 16], U16, "pos1_sb")
-        pos2_sb = held([P, PAIRS // 16], U16, "pos2_sb")
+        offs_sb = held([P, S // LIST_COL], U16, "offs_sb")
+        pos1_sb = held([P, PAIRS // LIST_COL], U16, "pos1_sb")
+        pos2_sb = held([P, PAIRS // LIST_COL], U16, "pos2_sb")
         tab_sc = held([P, T], U8, "tab_sc")
-        v_w = [held([P, S], U16, "v_w%d" % a) for a in range(2)]
-        v_sc = [held([P, S], U8, "v_sc%d" % a) for a in range(2)]
+        v_w = [held([P, S], U16, "v_w%d" % a) for a in range(K_PASSES)]
+        v_sc = [held([P, S], U8, "v_sc%d" % a) for a in range(K_PASSES)]
         w1_raw, w2_raw, w2_w, w2_sc = {}, {}, {}, {}
-        w1_bf = [[held([P, 4 * PASS], BF16, "w1_bf%d%d" % (b, a)) for a in range(2)] for b in range(2)]
-        w1_w = [[held([P, PASS], U32, "w1_w%d%d" % (b, a)) for a in range(2)] for b in range(2)]
-        w1_sc = [[held([P, PASS], U8, "w1_sc%d%d" % (b, a)) for a in range(2)] for b in range(2)]
-        w2_sc_raw = held([P, 2, H], U8, "w2_sc_raw")
-        b1_sb = held([P, 2, 4], F32, "b1_sb")
-        gain_sb = held([P, 2, 4], F32, "gain_sb")
-        gb_sb = held([P, 2, 4], F32, "gb_sb")
-        z_f = [held([P, 4, PAIRS], F32, "z_f%d" % b) for b in range(2)]
-        z_bf = [held([P, 4 * PAIRS], BF16, "z_bf%d" % b) for b in range(2)]
-        z_w = [held([P, PAIRS], U32, "z_w%d" % b) for b in range(2)]
-        z_sc = [held([P, PAIRS], U8, "z_sc%d" % b) for b in range(2)]
-        warm = held([P, 1], F32, "warm", "tab_w1")
+        w1_bf = [[held([P, PACK * PASS], BF16, "w1_bf%d%d" % (g, a)) for a in range(K_PASSES)] for g in range(R_PASSES)]
+        w1_w = [[held([P, PASS], U32, "w1_w%d%d" % (g, a)) for a in range(K_PASSES)] for g in range(R_PASSES)]
+        w1_sc = [[held([P, PASS], U8, "w1_sc%d%d" % (g, a)) for a in range(K_PASSES)] for g in range(R_PASSES)]
+        w2_sc_raw = held([P, K_PASSES, H], U8, "w2_sc_raw")
+        b1_sb = held([P, R_PASSES, PACK], F32, "b1_sb")
+        gain_sb = held([P, R_PASSES, PACK], F32, "gain_sb")
+        gain_b1 = held([P, R_PASSES, PACK], F32, "gain_b1")
+        z_f = [held([P, PACK, PAIRS], F32, "z_f%d" % g) for g in range(R_PASSES)]
+        z_bf = [held([P, PACK * PAIRS], BF16, "z_bf%d" % g) for g in range(R_PASSES)]
+        z_w = [held([P, PAIRS], U32, "z_w%d" % g) for g in range(R_PASSES)]
+        z_sc = [held([P, PAIRS], U8, "z_sc%d" % g) for g in range(R_PASSES)]
+        warm_in = held([P, 1], F32, "warm_in", "tab_w1")
         warm_out = held([P, 1], F32, "warm_out", "w1_raw0")
 
         nc.gpsimd.memset(tab_sc[:].bitcast(I32), 0)
         nc.vector.memset(w2_sc_raw[:].rearrange("p a c -> p (a c)").bitcast(I32), 0)
         nc.vector.memset(v_sc[1][:].bitcast(I32), 0)
-        nc.vector.memset(warm[:], 0.0)
-        nc.scalar.activation(out=warm_out[:], in_=warm[:], func=ACT.Tanh)
+        nc.vector.memset(warm_in[:], 0.0)
+        nc.scalar.activation(out=warm_out[:], in_=warm_in[:], func=ACT.Tanh)
 
-        tab_w = [held([P, T], U16, "tab_w%d" % a) for a in range(2)]
+        tab_w = [held([P, T], U16, "tab_w%d" % a) for a in range(K_PASSES)]
 
-        def load_w1(b, a):
-            src = w1[PASS * a : PASS * (a + 1), PASS * b : PASS * (b + 1)]
-            w1_raw[b, a] = held([P, 4, PASS], F32, "w1_raw%d%d" % (b, a), ("w1_raw0", "tab_w0")[a])
-            nc.sync.dma_start(out=w1_raw[b, a][:], in_=src.rearrange("(p j) c -> p j c", j=4))
+        def load_w1(g, a):
+            src = w1[PASS * a : PASS * (a + 1), PASS * g : PASS * (g + 1)]
+            w1_raw[g, a] = held([P, PACK, PASS], F32, "w1_raw%d%d" % (g, a), ("w1_raw0", "tab_w0")[a])
+            nc.sync.dma_start(out=w1_raw[g, a][:], in_=src.rearrange("(p j) c -> p j c", j=PACK))
 
-        def load_w2(b):
-            src = w2_words.rearrange("a p c i -> p a (c i)")[:, :, 4 * PASS * b : 4 * PASS * (b + 1)]
-            w2_raw[b] = held([P, 2, PASS], U32, "w2_raw%d" % b, "tab_sc")
-            nc.sync.dma_start(out=w2_raw[b][:].bitcast(I32), in_=src.bitcast(I32))
+        def load_w2(g):
+            src = w2_words.rearrange("a p c i -> p a (c i)")[:, :, PACK * PASS * g : PACK * PASS * (g + 1)]
+            w2_raw[g] = held([P, K_PASSES, PASS], U32, "w2_raw%d" % g, "tab_sc")
+            nc.sync.dma_start(out=w2_raw[g][:].bitcast(I32), in_=src.bitcast(I32))
 
-        def load_planes(dst, src, queue):
-            for q in range(4):
+        def load_scale_rows(dst, src, queue):
+            for q in range(QUADS):
                 queue.dma_start(
                     out=dst[32 * q : 32 * q + 4, :, :].bitcast(I32),
                     in_=src[:, 4 * q : 4 * q + 4, :].rearrange("a r c -> r a c").bitcast(I32),
@@ -84,62 +94,63 @@ def tile_list_duplicate_call_features_kernel(
         nc.sync.dma_start(pos1_sb[:], pos1)
         nc.sync.dma_start(pos2_sb[:], pos2)
         nc.sync.dma_start(out=tab_w[0][:].bitcast(I32), in_=tab_words[0].bitcast(I32))
-        nc.sync.dma_start(out=tab_sc[8:24, :].bitcast(I32), in_=tab_scales[1].bitcast(I32))
-        for q in range(4):
+        nc.sync.dma_start(out=tab_sc[SPARE_ROW : SPARE_ROW + 16, :].bitcast(I32), in_=tab_scales[1].bitcast(I32))
+        for q in range(QUADS):
             nc.sync.dma_start(out=tab_sc[32 * q : 32 * q + 4, :].bitcast(I32),
                               in_=tab_scales[0, 4 * q : 4 * q + 4, :].bitcast(I32))
         nc.sync.dma_start(out=tab_w[1][:].bitcast(I32), in_=tab_words[1].bitcast(I32))
         load_w1(0, 0)
-        load_planes(w2_sc_raw, w2_scales, nc.gpsimd)
-        nc.gpsimd.dma_start(out=b1_sb[:], in_=b1.rearrange("(b p t) -> p b t", b=2, t=4))
-        nc.gpsimd.dma_start(out=gain_sb[:], in_=gain.rearrange("(b p t) -> p b t", b=2, t=4))
+        load_scale_rows(w2_sc_raw, w2_scales, nc.gpsimd)
+        nc.gpsimd.dma_start(out=b1_sb[:], in_=b1.rearrange("(g p t) -> p g t", g=R_PASSES, t=PACK))
+        nc.gpsimd.dma_start(out=gain_sb[:], in_=gain.rearrange("(g p t) -> p g t", g=R_PASSES, t=PACK))
 
-        def cast_w1(b, a, m0, m1, engine):
-            dst = w1_bf[b][a][:].rearrange("p (t m j) -> p m j t", t=4, j=4)[:, m0:m1]
-            src = w1_raw[b, a][:].rearrange("p j (m t) -> p m j t", t=4)[:, m0:m1]
-            if engine == "scalar":
+        def round_w1(g, a, u, engine):
+            dst = w1_bf[g][a][:].rearrange("p (t m j) -> p m j t", t=PACK, j=PACK)[:, :, :, 2 * u : 2 * u + 2]
+            src = w1_raw[g, a][:].rearrange("p j (m t) -> p m j t", t=PACK)[:, :, :, 2 * u : 2 * u + 2]
+            if engine is nc.scalar:
                 nc.scalar.activation(out=dst, in_=src, func=ACT.Copy)
             else:
                 nc.vector.tensor_copy(out=dst, in_=src)
 
-        def quant_w1(b, a, t0, t1):
-            nc.vector.quantize_mx(out=w1_w[b][a][:, P * t0 : P * t1].bitcast(FP8X4), scales=w1_sc[b][a][:, P * t0 : P * t1],
-                                  in_=w1_bf[b][a][:, 4 * P * t0 : 4 * P * t1])
+        def quantise_w1(g, a, u):
+            cols = slice(2 * P * u, 2 * P * (u + 1))
+            nc.vector.quantize_mx(out=w1_w[g][a][:, cols].bitcast(FP8X4), scales=w1_sc[g][a][:, cols],
+                                  in_=w1_bf[g][a][:, PACK * cols.start : PACK * cols.stop])
 
-        def deal_w2_words(b):
-            w2_w[b] = held([P, 2, PASS], U32, "w2_w%d" % b, ("w1_bf00", "w2_w1")[b])
+        def deal_w2_words(g):
+            w2_w[g] = held([P, K_PASSES, PASS], U32, "w2_w%d" % g, ("w1_bf00", "w2_w1")[g])
             nc.vector.tensor_copy(
-                out=w2_w[b][:].rearrange("p a (t c i) -> p a c t i", t=4, i=4),
-                in_=w2_raw[b][:].rearrange("p a (c i t) -> p a c t i", t=4, i=4),
+                out=w2_w[g][:].rearrange("p a (u e m) -> p a u m e", u=2, e=2),
+                in_=w2_raw[g][:].rearrange("p a (m u e) -> p a u m e", u=2, e=2),
             )
 
-        def deal_w2_scales(b):
-            w2_sc[b] = held([P, 2, PASS], U8, "w2_sc%d" % b, ("tab_w1", "w1_bf01")[b])
+        def deal_w2_scales(g):
+            w2_sc[g] = held([P, K_PASSES, PASS], U8, "w2_sc%d" % g, ("tab_w1", "w1_bf01")[g])
             nc.vector.tensor_copy(
-                out=w2_sc[b][:].rearrange("p a (t m) -> p a t m", t=4),
-                in_=w2_sc_raw[:, :, PASS * b : PASS * (b + 1)].rearrange("p a (m t) -> p a t m", t=4),
+                out=w2_sc[g][:].rearrange("p a (t m) -> p a t m", t=PACK),
+                in_=w2_sc_raw[:, :, PASS * g : PASS * (g + 1)].rearrange("p a (m t) -> p a t m", t=PACK),
             )
 
         nc.vector.tensor_copy(v_w[0][:], tab_w[0][:].indirect(offs_sb[:]))
         load_w1(0, 1)
         nc.vector.tensor_copy(v_sc[0][:], tab_sc[:].indirect(offs_sb[:]))
-        for q in range(4):
+        for q in range(QUADS):
+            first = SPARE_ROW + 4 * q
             nc.sync.dma_start(out=v_sc[1][32 * q : 32 * q + 4, :].bitcast(I32),
-                              in_=v_sc[0][8 + 4 * q : 12 + 4 * q, :].bitcast(I32))
+                              in_=v_sc[0][first : first + 4, :].bitcast(I32))
         load_w2(0)
-        cast_w1(0, 0, 0, P, "scalar")
+        round_w1(0, 0, 0, nc.scalar)
+        round_w1(0, 0, 1, nc.scalar)
         nc.vector.tensor_copy(v_w[1][:], tab_w[1][:].indirect(offs_sb[:]))
         deal_w2_scales(0)
-        cast_w1(0, 1, 0, 40, "scalar")
-        cast_w1(0, 1, 40, P, "vector")
-        quant_w1(0, 0, 0, 1)
-        quant_w1(0, 1, 0, 1)
-        quant_w1(0, 0, 1, 2)
-        quant_w1(0, 0, 2, 4)
+        quantise_w1(0, 0, 0)
+        round_w1(0, 1, 0, nc.vector)
+        round_w1(0, 1, 1, nc.scalar)
+        quantise_w1(0, 0, 1)
+        quantise_w1(0, 1, 0)
         deal_w2_words(0)
-        quant_w1(0, 1, 1, 2)
-        quant_w1(0, 1, 2, 4)
-        nc.gpsimd.tensor_tensor(gb_sb[:], gain_sb[:], b1_sb[:], ALU.mult)
+        quantise_w1(0, 1, 1)
+        nc.gpsimd.tensor_tensor(gain_b1[:], gain_sb[:], b1_sb[:], ALU.mult)
 
         load_w1(1, 0)
         load_w1(1, 1)
@@ -147,112 +158,113 @@ def tile_list_duplicate_call_features_kernel(
 
         def product(tag, words, scales, half):
             acc = psum.tile([P, BANK], F32, name=tag, tag=tag)
-            for a in range(2):
+            cols = slice(BANK * half, BANK * (half + 1))
+            for a in range(K_PASSES):
                 nc.tensor.matmul_mx(
                     out=acc[:], lhsT=words[a].bitcast(FP8X4), lhsT_scale=scales[a],
-                    rhs=v_w[a][:, BANK * half : BANK * (half + 1)].bitcast(FP4X4),
-                    rhs_scale=v_sc[a][:, BANK * half : BANK * (half + 1)],
-                    start=(a == 0), stop=(a == 1),
+                    rhs=v_w[a][:, cols].bitcast(FP4X4), rhs_scale=v_sc[a][:, cols],
+                    start=(a == 0), stop=(a == K_PASSES - 1),
                 )
             return acc
 
-        def first_stage(s):
-            b, t = divmod(s, 4)
+        def first_stage(g, t):
             cols = slice(P * t, P * (t + 1))
-            acc1 = [product("acc1_%d" % half, [w1_w[b][a][:, cols] for a in range(2)],
-                            [w1_sc[b][a][:, cols] for a in range(2)], half) for half in range(2)]
-            acc2 = [product("acc2_%d" % half, [w2_w[b][:, a, cols] for a in range(2)],
-                            [w2_sc[b][:, a, cols] for a in range(2)], half) for half in range(2)]
+            halves = range(S // BANK)
+            acc1 = [product("acc1_%d" % half, [w1_w[g][a][:, cols] for a in range(K_PASSES)],
+                            [w1_sc[g][a][:, cols] for a in range(K_PASSES)], half) for half in halves]
+            acc2 = [product("acc2_%d" % half, [w2_w[g][:, a, cols] for a in range(K_PASSES)],
+                            [w2_sc[g][:, a, cols] for a in range(K_PASSES)], half) for half in halves]
             rows = ring.tile([P, 2 * S], F32, name="rows")
-            th = ring.tile([P, S], F32, name="th")
-            for half in range(2):
+            tanh_h = ring.tile([P, S], F32, name="tanh_h")
+            for half in halves:
                 cs = slice(BANK * half, BANK * (half + 1))
-                nc.scalar.activation(out=th[:, cs], in_=acc1[half][:], func=ACT.Tanh, bias=b1_sb[:, b, t : t + 1])
-            for half in range(2):
+                nc.scalar.activation(out=tanh_h[:, cs], in_=acc1[half][:], func=ACT.Tanh, bias=b1_sb[:, g, t : t + 1])
+            for half in halves:
                 cs = slice(S + BANK * half, S + BANK * (half + 1))
                 nc.scalar.activation(out=rows[:, cs], in_=acc1[half][:], func=ACT.Identity,
-                                     bias=gb_sb[:, b, t : t + 1], scale=gain_sb[:, b, t : t + 1])
-            for half in range(2):
+                                     bias=gain_b1[:, g, t : t + 1], scale=gain_sb[:, g, t : t + 1])
+            for half in halves:
                 cs = slice(BANK * half, BANK * (half + 1))
-                nc.vector.tensor_tensor(rows[:, cs], acc2[half][:], th[:, cs], ALU.add)
+                nc.vector.tensor_tensor(rows[:, cs], acc2[half][:], tanh_h[:, cs], ALU.add)
             early = ring.tile([P, PAIRS], F32, name="early")
             nc.vector.tensor_copy(early[:], rows[:, S : 2 * S].indirect(pos1_sb[:]))
             return rows, early
 
-        def pair_product(s, bb, early, m0=0, m1=PAIRS):
-            b, t = divmod(s, 4)
-            nc.vector.tensor_tensor(z_f[b][:, t, m0:m1], bb[:].indirect(pos2_sb[:, m0 // 16 : m1 // 16]),
-                                    early[:, m0:m1], ALU.mult)
-
-        def pair_product_apart(s, bb, early):
-            b, t = divmod(s, 4)
+        def pair_product(g, t, rows, early):
             late = ring.tile([P, PAIRS], F32, name="late")
-            nc.vector.tensor_copy(late[:], bb[:].indirect(pos2_sb[:]))
-            nc.gpsimd.tensor_tensor(z_f[b][:, t, :], late[:], early[:], ALU.mult)
+            nc.vector.tensor_copy(late[:], rows[:].indirect(pos2_sb[:]))
+            nc.gpsimd.tensor_tensor(z_f[g][:, t, :], late[:], early[:], ALU.mult)
 
-        def weave_z(b, c0, c1, engine):
-            dst = z_bf[b][:].rearrange("p (c i t) -> p c t i", i=4, t=4)[:, c0:c1]
-            src = z_f[b][:].rearrange("p t (c i) -> p c t i", i=4)[:, c0:c1]
-            if engine == "scalar":
-                nc.scalar.activation(out=dst, in_=src, func=ACT.Copy)
-            else:
-                nc.vector.tensor_copy(out=dst, in_=src)
+        def round_z(g, m0, m1):
+            nc.scalar.activation(
+                out=z_bf[g][:].rearrange("p (c i t) -> p c t i", i=4, t=PACK)[:, m0 // 4 : m1 // 4],
+                in_=z_f[g][:].rearrange("p t (c i) -> p c t i", i=4)[:, m0 // 4 : m1 // 4],
+                func=ACT.Copy,
+            )
 
-        def quant_z(b, m0=0, m1=PAIRS):
-            nc.vector.quantize_mx(out=z_w[b][:, m0:m1].bitcast(FP8X4), scales=z_sc[b][:, m0:m1],
-                                  in_=z_bf[b][:, 4 * m0 : 4 * m1])
+        def quantise_z(g, m0, m1):
+            nc.vector.quantize_mx(out=z_w[g][:, m0:m1].bitcast(FP8X4), scales=z_sc[g][:, m0:m1],
+                                  in_=z_bf[g][:, PACK * m0 : PACK * m1])
 
-        for s in range(8):
-            pending = first_stage(s)
-            if s < 7:
-                pair_product_apart(s, *pending)
-            if s < 4:
-                cast_w1(1, s // 2, 64 * (s % 2), 64 * (s % 2 + 1), "scalar")
+        for s in range(SLICES):
+            g, t = divmod(s, PACK)
+            rows, early = first_stage(g, t)
+            if s < SLICES - 1:
+                pair_product(g, t, rows, early)
+            if g == 0:
+                u, a = divmod(t, K_PASSES)
+                round_w1(1, a, u, nc.scalar)
+                quantise_w1(1, a, u)
             if s == 0:
                 deal_w2_scales(1)
             if s == 1:
                 deal_w2_words(1)
-            if s in (2, 3):
-                quant_w1(1, s - 2, 0, 4)
-            if s == 3:
-                w3_w = held([P, 2, 2 * N], U8, "w3_w", "w1_bf10")
-                nc.sync.dma_start(out=w3_w[:].bitcast(I32), in_=w3_words.rearrange("a p c -> p a c").bitcast(I32))
-                w3_sc = held([P, 2, N], U8, "w3_sc", "w1_bf11")
-                nc.vector.memset(w3_sc[:].rearrange("p a c -> p (a c)").bitcast(I32), 0)
-                load_planes(w3_sc, w3_scales, nc.sync)
-                dist_sb = held([P, 4, PAIRS], F32, "dist_sb", "w1_raw0")
+            if s == PACK - 1:
+                w3_w = held([P, R_PASSES, 2 * N], U8, "w3_w", "w1_bf10")
+                nc.sync.dma_start(out=w3_w[:].bitcast(I32), in_=w3_words.rearrange("g p c -> p g c").bitcast(I32))
+                w3_sc = held([P, R_PASSES, N], U8, "w3_sc", "w1_bf11")
+                nc.gpsimd.memset(w3_sc[:].rearrange("p g c -> p (g c)").bitcast(I32), 0)
+                load_scale_rows(w3_sc, w3_scales, nc.sync)
+                dist_sb = held([P, N // P, PAIRS], F32, "dist_sb", "w1_raw0")
                 nc.sync.dma_start(out=dist_sb[:], in_=district.rearrange("(c p) m -> p c m", p=P))
-            if s in (4, 5):
-                weave_z(0, 64 * (s - 4), 64 * (s - 3), "scalar")
-            if s == 6:
-                quant_z(0)
+            if g == 1 and t < 2:
+                round_z(0, t * PAIRS // 2, (t + 1) * PAIRS // 2)
+            if g == 1 and t == 2:
+                quantise_z(0, 0, PAIRS)
+
         tags = ["acc1_0", "acc1_1", "acc2_0", "acc2_1"]
-        feats = [psum.tile([P, 4, P], F32, name=tags[u], tag=tags[u]) for u in range(4)]
+        feats = [psum.tile([P, N // P, CHUNK], F32, name=tags[u], tag=tags[u]) for u in range(CHUNKS)]
         out_v = out.rearrange("(c p) m -> p c m", p=P)
 
-        def last_pass(b, u):
-            for c in range(4):
+        def last_pass(g, u):
+            pairs = slice(CHUNK * u, CHUNK * (u + 1))
+            for c in range(N // P):
                 nc.tensor.matmul_mx(
-                    out=feats[u][:, c, :], lhsT=w3_w[:, b, 2 * P * c : 2 * P * (c + 1)].bitcast(FP4X4),
-                    lhsT_scale=w3_sc[:, b, P * c : P * (c + 1)],
-                    rhs=z_w[b][:, P * u : P * (u + 1)].bitcast(FP8X4), rhs_scale=z_sc[b][:, P * u : P * (u + 1)],
-                    start=(b == 0 and c == 0), stop=(b == 1 and c == 3),
+                    out=feats[u][:, c, :], lhsT=w3_w[:, g, 2 * P * c : 2 * P * (c + 1)].bitcast(FP4X4),
+                    lhsT_scale=w3_sc[:, g, P * c : P * (c + 1)],
+                    rhs=z_w[g][:, pairs].bitcast(FP8X4), rhs_scale=z_sc[g][:, pairs],
+                    start=(g == 0 and c == 0), stop=(g == R_PASSES - 1 and c == N // P - 1),
                 )
 
         def finish(u):
-            res = ring.tile([P, 4, P], F32, name="res", bufs=4)
-            nc.vector.tensor_tensor(res[:], feats[u][:], dist_sb[:, :, P * u : P * (u + 1)], ALU.add)
-            nc.sync.dma_start(out=out_v[:, :, P * u : P * (u + 1)], in_=res[:])
+            pairs = slice(CHUNK * u, CHUNK * (u + 1))
+            res = ring.tile([P, N // P, CHUNK], F32, name="res", bufs=CHUNKS)
+            nc.vector.tensor_tensor(res[:], feats[u][:], dist_sb[:, :, pairs], ALU.add)
+            nc.sync.dma_start(out=out_v[:, :, pairs], in_=res[:])
 
-        for u in range(4):
+        for u in range(CHUNKS):
             last_pass(0, u)
-        for step in range(7):
-            if step < 4:
-                pair_product(7, *pending, P * step, P * (step + 1))
-                weave_z(1, 32 * step, 32 * (step + 1), "scalar")
-            if 1 <= step < 5:
-                u = step - 1
-                quant_z(1, P * u, P * (u + 1))
+        quantise_lag, finish_lag = 1, 3
+        for step in range(CHUNKS + finish_lag):
+            if step < CHUNKS:
+                m0, m1 = CHUNK * step, CHUNK * (step + 1)
+                nc.vector.tensor_tensor(z_f[1][:, PACK - 1, m0:m1],
+                                        rows[:].indirect(pos2_sb[:, m0 // LIST_COL : m1 // LIST_COL]),
+                                        early[:, m0:m1], ALU.mult)
+                round_z(1, m0, m1)
+            if quantise_lag <= step < CHUNKS + quantise_lag:
+                u = step - quantise_lag
+                quantise_z(1, CHUNK * u, CHUNK * (u + 1))
                 last_pass(1, u)
-            if step >= 3:
-                finish(step - 3)
+            if step >= finish_lag:
+                finish(step - finish_lag)

from contextlib import ExitStack

import concourse.mybir as mybir

K, T, S, H, PAIRS, N = 1024, 4096, 1024, 1024, 512, 512
FLOPS = 2 * (2 * K * H * S) + 2 * H * N * PAIRS

F32 = mybir.dt.float32
BF16 = mybir.dt.bfloat16
I32 = mybir.dt.int32
U32 = mybir.dt.uint32
U16 = mybir.dt.uint16
U8 = mybir.dt.uint8
FP8X4 = mybir.dt.float8_e4m3fn_x4
FP4X4 = mybir.dt.float4_e2m1fn_x4
ACT = mybir.ActivationFunctionType
ALU = mybir.AluOpType

P = 128
PACK = 4
PASS = P * PACK
K_PASSES = K // PASS
R_PASSES = H // PASS
SLICES = R_PASSES * PACK
QUADS = 4
BANK = 512
LIST_COL = 16
SPARE_ROW = 8
CHUNK = 128
CHUNKS = PAIRS // CHUNK
RING = 3


def tile_list_duplicate_call_features_kernel(
    tc, tab_words, tab_scales, offs, w1, b1, w2_words, w2_scales, pos1, pos2,
    gain, w3_words, w3_scales, district, out,
):
    nc = tc.nc
    with ExitStack() as ctx:
        keep = ctx.enter_context(tc.tile_pool(name="keep", bufs=1))
        ring = ctx.enter_context(tc.tile_pool(name="ring", bufs=RING))
        psum = ctx.enter_context(tc.psum_pool(name="psum", bufs=2))

        def held(shape, dtype, name, on_bytes_of=""):
            return keep.tile(shape, dtype, name=name, tag=on_bytes_of or name, align_bytes=64)

        offs_sb = held([P, S // LIST_COL], U16, "offs_sb")
        pos1_sb = held([P, PAIRS // LIST_COL], U16, "pos1_sb")
        pos2_sb = held([P, PAIRS // LIST_COL], U16, "pos2_sb")
        tab_sc = held([P, T], U8, "tab_sc")
        v_w = [held([P, S], U16, "v_w%d" % a) for a in range(K_PASSES)]
        v_sc = [held([P, S], U8, "v_sc%d" % a) for a in range(K_PASSES)]
        w1_raw, w2_raw, w2_w, w2_sc = {}, {}, {}, {}
        w1_bf = [[held([P, PACK * PASS], BF16, "w1_bf%d%d" % (g, a)) for a in range(K_PASSES)] for g in range(R_PASSES)]
        w1_w = [[held([P, PASS], U32, "w1_w%d%d" % (g, a)) for a in range(K_PASSES)] for g in range(R_PASSES)]
        w1_sc = [[held([P, PASS], U8, "w1_sc%d%d" % (g, a)) for a in range(K_PASSES)] for g in range(R_PASSES)]
        w2_sc_raw = held([P, K_PASSES, H], U8, "w2_sc_raw")
        b1_sb = held([P, R_PASSES, PACK], F32, "b1_sb")
        gain_sb = held([P, R_PASSES, PACK], F32, "gain_sb")
        gain_b1 = held([P, R_PASSES, PACK], F32, "gain_b1")
        z_f = [held([P, PACK, PAIRS], F32, "z_f%d" % g) for g in range(R_PASSES)]
        z_bf = [held([P, PACK * PAIRS], BF16, "z_bf%d" % g) for g in range(R_PASSES)]
        z_w = [held([P, PAIRS], U32, "z_w%d" % g) for g in range(R_PASSES)]
        z_sc = [held([P, PAIRS], U8, "z_sc%d" % g) for g in range(R_PASSES)]
        warm_in = held([P, 1], F32, "warm_in", "tab_w1")
        warm_out = held([P, 1], F32, "warm_out", "w1_raw0")

        nc.gpsimd.memset(tab_sc[:].bitcast(I32), 0)
        nc.vector.memset(w2_sc_raw[:].rearrange("p a c -> p (a c)").bitcast(I32), 0)
        nc.vector.memset(v_sc[1][:].bitcast(I32), 0)
        nc.vector.memset(warm_in[:], 0.0)
        nc.scalar.activation(out=warm_out[:], in_=warm_in[:], func=ACT.Tanh)

        tab_w = [held([P, T], U16, "tab_w%d" % a) for a in range(K_PASSES)]

        def load_w1(g, a):
            src = w1[PASS * a : PASS * (a + 1), PASS * g : PASS * (g + 1)]
            w1_raw[g, a] = held([P, PACK, PASS], F32, "w1_raw%d%d" % (g, a), ("w1_raw0", "tab_w0")[a])
            nc.sync.dma_start(out=w1_raw[g, a][:], in_=src.rearrange("(p j) c -> p j c", j=PACK))

        def load_w2(g):
            src = w2_words.rearrange("a p c i -> p a (c i)")[:, :, PACK * PASS * g : PACK * PASS * (g + 1)]
            w2_raw[g] = held([P, K_PASSES, PASS], U32, "w2_raw%d" % g, "tab_sc")
            nc.sync.dma_start(out=w2_raw[g][:].bitcast(I32), in_=src.bitcast(I32))

        def load_scale_rows(dst, src, queue):
            for q in range(QUADS):
                queue.dma_start(
                    out=dst[32 * q : 32 * q + 4, :, :].bitcast(I32),
                    in_=src[:, 4 * q : 4 * q + 4, :].rearrange("a r c -> r a c").bitcast(I32),
                )

        nc.sync.dma_start(offs_sb[:], offs)
        nc.sync.dma_start(pos1_sb[:], pos1)
        nc.sync.dma_start(pos2_sb[:], pos2)
        nc.sync.dma_start(out=tab_w[0][:].bitcast(I32), in_=tab_words[0].bitcast(I32))
        nc.sync.dma_start(out=tab_sc[SPARE_ROW : SPARE_ROW + 16, :].bitcast(I32), in_=tab_scales[1].bitcast(I32))
        for q in range(QUADS):
            nc.sync.dma_start(out=tab_sc[32 * q : 32 * q + 4, :].bitcast(I32),
                              in_=tab_scales[0, 4 * q : 4 * q + 4, :].bitcast(I32))
        nc.sync.dma_start(out=tab_w[1][:].bitcast(I32), in_=tab_words[1].bitcast(I32))
        load_w1(0, 0)
        load_scale_rows(w2_sc_raw, w2_scales, nc.gpsimd)
        nc.gpsimd.dma_start(out=b1_sb[:], in_=b1.rearrange("(g p t) -> p g t", g=R_PASSES, t=PACK))
        nc.gpsimd.dma_start(out=gain_sb[:], in_=gain.rearrange("(g p t) -> p g t", g=R_PASSES, t=PACK))

        def round_w1(g, a, u, engine):
            dst = w1_bf[g][a][:].rearrange("p (t m j) -> p m j t", t=PACK, j=PACK)[:, :, :, 2 * u : 2 * u + 2]
            src = w1_raw[g, a][:].rearrange("p j (m t) -> p m j t", t=PACK)[:, :, :, 2 * u : 2 * u + 2]
            if engine is nc.scalar:
                nc.scalar.activation(out=dst, in_=src, func=ACT.Copy)
            else:
                nc.vector.tensor_copy(out=dst, in_=src)

        def quantise_w1(g, a, u):
            cols = slice(2 * P * u, 2 * P * (u + 1))
            nc.vector.quantize_mx(out=w1_w[g][a][:, cols].bitcast(FP8X4), scales=w1_sc[g][a][:, cols],
                                  in_=w1_bf[g][a][:, PACK * cols.start : PACK * cols.stop])

        def deal_w2_words(g):
            w2_w[g] = held([P, K_PASSES, PASS], U32, "w2_w%d" % g, ("w1_bf00", "w2_w1")[g])
            nc.vector.tensor_copy(
                out=w2_w[g][:].rearrange("p a (u e m) -> p a u m e", u=2, e=2),
                in_=w2_raw[g][:].rearrange("p a (m u e) -> p a u m e", u=2, e=2),
            )

        def deal_w2_scales(g):
            w2_sc[g] = held([P, K_PASSES, PASS], U8, "w2_sc%d" % g, ("tab_w1", "w1_bf01")[g])
            nc.vector.tensor_copy(
                out=w2_sc[g][:].rearrange("p a (t m) -> p a t m", t=PACK),
                in_=w2_sc_raw[:, :, PASS * g : PASS * (g + 1)].rearrange("p a (m t) -> p a t m", t=PACK),
            )

        nc.vector.tensor_copy(v_w[0][:], tab_w[0][:].indirect(offs_sb[:]))
        load_w1(0, 1)
        nc.vector.tensor_copy(v_sc[0][:], tab_sc[:].indirect(offs_sb[:]))
        for q in range(QUADS):
            first = SPARE_ROW + 4 * q
            nc.sync.dma_start(out=v_sc[1][32 * q : 32 * q + 4, :].bitcast(I32),
                              in_=v_sc[0][first : first + 4, :].bitcast(I32))
        load_w2(0)
        round_w1(0, 0, 0, nc.scalar)
        round_w1(0, 0, 1, nc.scalar)
        nc.vector.tensor_copy(v_w[1][:], tab_w[1][:].indirect(offs_sb[:]))
        deal_w2_scales(0)
        quantise_w1(0, 0, 0)
        round_w1(0, 1, 0, nc.vector)
        round_w1(0, 1, 1, nc.scalar)
        quantise_w1(0, 0, 1)
        quantise_w1(0, 1, 0)
        deal_w2_words(0)
        quantise_w1(0, 1, 1)
        nc.gpsimd.tensor_tensor(gain_b1[:], gain_sb[:], b1_sb[:], ALU.mult)

        load_w1(1, 0)
        load_w1(1, 1)
        load_w2(1)

        def product(tag, words, scales, half):
            acc = psum.tile([P, BANK], F32, name=tag, tag=tag)
            cols = slice(BANK * half, BANK * (half + 1))
            for a in range(K_PASSES):
                nc.tensor.matmul_mx(
                    out=acc[:], lhsT=words[a].bitcast(FP8X4), lhsT_scale=scales[a],
                    rhs=v_w[a][:, cols].bitcast(FP4X4), rhs_scale=v_sc[a][:, cols],
                    start=(a == 0), stop=(a == K_PASSES - 1),
                )
            return acc

        def first_stage(g, t):
            cols = slice(P * t, P * (t + 1))
            halves = range(S // BANK)
            acc1 = [product("acc1_%d" % half, [w1_w[g][a][:, cols] for a in range(K_PASSES)],
                            [w1_sc[g][a][:, cols] for a in range(K_PASSES)], half) for half in halves]
            acc2 = [product("acc2_%d" % half, [w2_w[g][:, a, cols] for a in range(K_PASSES)],
                            [w2_sc[g][:, a, cols] for a in range(K_PASSES)], half) for half in halves]
            rows = ring.tile([P, 2 * S], F32, name="rows")
            tanh_h = ring.tile([P, S], F32, name="tanh_h")
            for half in halves:
                cs = slice(BANK * half, BANK * (half + 1))
                nc.scalar.activation(out=tanh_h[:, cs], in_=acc1[half][:], func=ACT.Tanh, bias=b1_sb[:, g, t : t + 1])
            for half in halves:
                cs = slice(S + BANK * half, S + BANK * (half + 1))
                nc.scalar.activation(out=rows[:, cs], in_=acc1[half][:], func=ACT.Identity,
                                     bias=gain_b1[:, g, t : t + 1], scale=gain_sb[:, g, t : t + 1])
            for half in halves:
                cs = slice(BANK * half, BANK * (half + 1))
                nc.vector.tensor_tensor(rows[:, cs], acc2[half][:], tanh_h[:, cs], ALU.add)
            early = ring.tile([P, PAIRS], F32, name="early")
            nc.vector.tensor_copy(early[:], rows[:, S : 2 * S].indirect(pos1_sb[:]))
            return rows, early

        def pair_product(g, t, rows, early):
            late = ring.tile([P, PAIRS], F32, name="late")
            nc.vector.tensor_copy(late[:], rows[:].indirect(pos2_sb[:]))
            nc.gpsimd.tensor_tensor(z_f[g][:, t, :], late[:], early[:], ALU.mult)

        def round_z(g, m0, m1):
            nc.scalar.activation(
                out=z_bf[g][:].rearrange("p (c i t) -> p c t i", i=4, t=PACK)[:, m0 // 4 : m1 // 4],
                in_=z_f[g][:].rearrange("p t (c i) -> p c t i", i=4)[:, m0 // 4 : m1 // 4],
                func=ACT.Copy,
            )

        def quantise_z(g, m0, m1):
            nc.vector.quantize_mx(out=z_w[g][:, m0:m1].bitcast(FP8X4), scales=z_sc[g][:, m0:m1],
                                  in_=z_bf[g][:, PACK * m0 : PACK * m1])

        for s in range(SLICES):
            g, t = divmod(s, PACK)
            rows, early = first_stage(g, t)
            if s < SLICES - 1:
                pair_product(g, t, rows, early)
            if g == 0:
                u, a = divmod(t, K_PASSES)
                round_w1(1, a, u, nc.scalar)
                quantise_w1(1, a, u)
            if s == 0:
                deal_w2_scales(1)
            if s == 1:
                deal_w2_words(1)
            if s == PACK - 1:
                w3_w = held([P, R_PASSES, 2 * N], U8, "w3_w", "w1_bf10")
                nc.sync.dma_start(out=w3_w[:].bitcast(I32), in_=w3_words.rearrange("g p c -> p g c").bitcast(I32))
                w3_sc = held([P, R_PASSES, N], U8, "w3_sc", "w1_bf11")
                nc.gpsimd.memset(w3_sc[:].rearrange("p g c -> p (g c)").bitcast(I32), 0)
                load_scale_rows(w3_sc, w3_scales, nc.sync)
                dist_sb = held([P, N // P, PAIRS], F32, "dist_sb", "w1_raw0")
                nc.sync.dma_start(out=dist_sb[:], in_=district.rearrange("(c p) m -> p c m", p=P))
            if g == 1 and t < 2:
                round_z(0, t * PAIRS // 2, (t + 1) * PAIRS // 2)
            if g == 1 and t == 2:
                quantise_z(0, 0, PAIRS)

        tags = ["acc1_0", "acc1_1", "acc2_0", "acc2_1"]
        feats = [psum.tile([P, N // P, CHUNK], F32, name=tags[u], tag=tags[u]) for u in range(CHUNKS)]
        out_v = out.rearrange("(c p) m -> p c m", p=P)

        def last_pass(g, u):
            pairs = slice(CHUNK * u, CHUNK * (u + 1))
            for c in range(N // P):
                nc.tensor.matmul_mx(
                    out=feats[u][:, c, :], lhsT=w3_w[:, g, 2 * P * c : 2 * P * (c + 1)].bitcast(FP4X4),
                    lhsT_scale=w3_sc[:, g, P * c : P * (c + 1)],
                    rhs=z_w[g][:, pairs].bitcast(FP8X4), rhs_scale=z_sc[g][:, pairs],
                    start=(g == 0 and c == 0), stop=(g == R_PASSES - 1 and c == N // P - 1),
                )

        def finish(u):
            pairs = slice(CHUNK * u, CHUNK * (u + 1))
            res = ring.tile([P, N // P, CHUNK], F32, name="res", bufs=CHUNKS)
            nc.vector.tensor_tensor(res[:], feats[u][:], dist_sb[:, :, pairs], ALU.add)
            nc.sync.dma_start(out=out_v[:, :, pairs], in_=res[:])

        for u in range(CHUNKS):
            last_pass(0, u)
        quantise_lag, finish_lag = 1, 3
        for step in range(CHUNKS + finish_lag):
            if step < CHUNKS:
                m0, m1 = CHUNK * step, CHUNK * (step + 1)
                nc.vector.tensor_tensor(z_f[1][:, PACK - 1, m0:m1],
                                        rows[:].indirect(pos2_sb[:, m0 // LIST_COL : m1 // LIST_COL]),
                                        early[:, m0:m1], ALU.mult)
                round_z(1, m0, m1)
            if quantise_lag <= step < CHUNKS + quantise_lag:
                u = step - quantise_lag
                quantise_z(1, CHUNK * u, CHUNK * (u + 1))
                last_pass(1, u)
            if step >= finish_lag:
                finish(step - finish_lag)
